import numpy as np
CORES = [21,109,149,237,277,365,405,493,150,406]
N = 10
TK = 256
D = 128 * N
EPS = 0.01
def setup_inputs(rng):
    return {"x": (rng.standard_normal((N, 128, TK), dtype=np.float32) * (0.5 + np.abs(rng.standard_normal((1, 1, TK), dtype=np.float32))) + rng.standard_normal((1, 1, TK), dtype=np.float32)), "w": (rng.standard_normal((N, 128, 128), dtype=np.float32) / 11)}
def reference(x, w):
    X = x.astype(np.float64)
    mu = X.sum(axis=(0, 1)) / D
    Z = X - mu
    Z = Z / np.sqrt((Z ** 2).sum(axis=(0, 1)) / D + EPS)
    s = sum(w[r].astype(np.float64).T @ Z[r] for r in range(N)).astype(np.float32)
    return {"y": np.broadcast_to(s, (N,) + s.shape)}

from concourse.bass import DstId, RemoteDMATransfer
from concourse.mybir import AluOpType, ActivationFunctionType

TK = 256
D = 1280
EPS = 0.01
W = 64
NS = 5

SCRATCH = {
    "xs": ("sbuf", [128, TK], "float32"),
    "xq": ("sbuf", [128, TK], "float32"),
    "ws": ("sbuf", [128, 128], "float32"),
    "on1": ("sbuf", [128, 128], "float32"),
    "idn": ("sbuf", [128, 128], "float32"),
    "ss": ("sbuf", [128, NS], "float32"),
    "sb": ("sbuf", [128, TK], "float32"),
    "sp": ("sbuf", [128, 4 * NS], "float32"),
    "t1": ("sbuf", [128, 2 * NS], "float32"),
    "t2": ("sbuf", [128, NS], "float32"),
    "mu": ("sbuf", [128, 2], "float32"),
    "m2": ("sbuf", [128, 2], "float32"),
    "ve": ("sbuf", [128, 2], "float32"),
    "va": ("sbuf", [128, 2], "float32"),
    "sd": ("sbuf", [128, 2], "float32"),
    "rs": ("sbuf", [128, 2], "float32"),
    "dgm": ("sbuf", [128, TK], "float32"),
    "dgr": ("sbuf", [128, TK], "float32"),
    "acc": ("sbuf", [128, TK], "float32"),
    "u": ("sbuf", [128, TK], "float32"),
    "yo": ("sbuf", [128, TK], "float32"),
    "pS": ("psum", [128, 512], "float32"),
    "pA0": ("psum", [128, 512], "float32"),
    "pA1": ("psum", [128, 512], "float32"),
    "pM": ("psum", [128, 512], "float32"),
    "pG": ("psum", [128, 512], "float32"),
    "pB": ("psum", [128, 512], "float32"),
    "l1s": ("dram", [3, 128, NS], "float32"),
    "l1": ("dram", [3, 128, W], "float32"),
    "l2": ("dram", [3, 128, W], "float32"),
}
SEMAPHORES = ["ldx", "ldw", "cst", "idr", "sq", "pe1", "sc", "pa0", "pa1", "mc", "snt", "s1", "m1", "m2", "st",
              "m3a", "m3b", "v1", "v2", "v3", "v4", "v5", "v6", "dm", "pm", "vg", "sqd", "rsr", "dr0", "dr1", "pb",
              "ua", "ub", "ya", "yb", "sta", "stb"]

_CACHE = {}


def _bits(m):
    return [b for b in range(m.bit_length()) if (m >> b) & 1]


def _part(m, k, n):
    b = _bits(m)
    s = len(b) // n
    r = 0
    for e in b[k * s:(k + 1) * s]:
        r |= 1 << e
    return r


def _plan(T, topo):
    if "p" in _CACHE:
        return _CACHE["p"]
    ranks = list(T.cores)
    n = topo.CORES_PER_CHIP

    def key(c):
        return (topo.host(c), topo.chip(c))

    chips = sorted(set(key(c) for c in ranks))
    on = {k: [c for c in ranks if key(c) == k] for k in chips}
    rep = {k: on[k][0] for k in chips}
    cores = {k: [x for x in range(max(0, rep[k] - n + 1), rep[k] + n) if key(x) == k] for k in chips}

    def reach(a, b):
        return any(topo.may_write(x, rep[b]) for x in cores[a])

    peer, partner, holders = {}, {}, {}
    for k in chips:
        peer[k] = [b for b in chips if b != k and topo.same_plane(rep[k], rep[b])][0]
        partner[k[0]] = [b[0] for b in chips if topo.rack(b[0]) != topo.rack(k[0]) and reach(k, b)][0]
        own = [x for x in cores[k] if x not in ranks
               and all(topo.may_write(x, rep[b]) for b in chips if b != k and reach(k, b))]
        d0 = topo.die(rep[k])
        dies = [d0] + sorted(set(topo.die(x) for x in own if topo.die(x) != d0))
        holders[k] = [max(x for x in own if topo.die(x) == d) for d in dies][:2]
    pairs = sorted(set(tuple(sorted((h, partner[h]))) for h in partner))
    pidx = {h: pairs.index(tuple(sorted((h, partner[h])))) for h in partner}
    four = {h: [b for b in chips if b[0] in (h, partner[h])] for h in partner}
    group = {k: [c for c in ranks if key(c) in (k, peer[k])] for k in chips}
    role = {}
    for k in chips:
        for i, x in enumerate(holders[k]):
            role[x] = (k, i)
    p = dict(ranks=ranks, key=key, chips=chips, on=on, peer=peer, partner=partner, holders=holders, pidx=pidx,
             four=four, group=group, role=role)
    _CACHE["p"] = p
    return p


def _masks(topo, core, far, near):
    off = topo.mask(core, far)
    return off, topo.mask(core, near) & ~off


def _stat_dests(P, k, i):
    far = [r for r in P["ranks"] if P["key"](r) != k and P["key"](r)[0] in (k[0], P["partner"][k[0]])]
    return far[i::2], P["on"][k][i::2]


def _holder(g, core, T, topo, P):
    S = T.sem
    k, i = P["role"][core]
    key, holders, peer = P["key"], P["holders"], P["peer"]
    grp = P["group"][k]
    ns = len(grp)
    off, onm = _masks(topo, core, P["on"][peer[k]][0], P["on"][k][0])
    sent = 0

    def dst(d):
        rid, pid = topo.addr(d, core)
        return DstId(rid=rid, pnc=pid)

    def cnt_from(r, n):
        o, m = _masks(topo, r, holders[peer[key(r)]][0], holders[key(r)][0])
        return len(_bits(m if key(r) == k else o)) // n

    g.wait_ge(S.s1, sum(cnt_from(r, 1) for r in grp))
    far, near = _stat_dests(P, k, i)
    tr = []
    for dl, m in ((far, off), (near, onm)):
        if dl:
            cols = [P["four"][key(d)[0]].index(k) * NS for d in dl]
            tr.append(RemoteDMATransfer(dst_ids=[dst(d) for d in dl], dma_engine_mask=m, remote_sem=S.st,
                                        srcs=[T.l1s[s] for s in range(ns)],
                                        dsts=[T.sp[:, c:c + NS] for c in cols], alu_op=1))
            sent += len(_bits(m))
    g.remote_dma_fused(tr, local_sem=S.snt)

    g.wait_ge(S.m1, sum(cnt_from(r, 2) for r in grp))
    others = [b for b in P["four"][k[0]] if b != k]
    slots = [[a for a in P["four"][b[0]] if a != b].index(k) for b in others]
    g.remote_dma_fused([RemoteDMATransfer(dst_ids=[dst(holders[b][i]) for b in others], dma_engine_mask=off,
                                          remote_sem=S.m2, srcs=[T.l1[s] for s in range(ns)],
                                          dsts=[T.l2[s] for s in slots], alu_op=1)], local_sem=S.snt)
    sent += len(_bits(off))

    g.wait_ge(S.m2, len(others) * len(_bits(off)))
    q = (2 * P["pidx"][k[0]] + i) * W
    src = [T.l1[s] for s in range(ns)] + [T.l2[s] for s in range(len(others))]
    tr = []
    for dl, m, sem in ((P["on"][peer[k]], off, S.m3b), (P["on"][k], onm, S.m3a)):
        tr.append(RemoteDMATransfer(dst_ids=[dst(d) for d in dl], dma_engine_mask=m, remote_sem=sem, srcs=src,
                                    dsts=[T.acc[:, q:q + W] for d in dl], alu_op=1))
        sent += len(_bits(m))
    g.remote_dma_fused(tr, local_sem=S.snt)
    g.wait_ge(S.snt, sent)


def _rank(g, core, T, topo, P):
    S = T.sem
    A, F = AluOpType, ActivationFunctionType
    v, pe, act, sy = g.vector, g.tensor, g.scalar, g.sync
    key, holders = P["key"], P["holders"]
    k = key(core)
    pk = P["peer"][k]
    slot = P["group"][k].index(core)
    off, onm = _masks(topo, core, holders[pk][0], holders[k][0])
    one = T.on1[:, 0:1]

    def dst(d):
        rid, pid = topo.addr(d, core)
        return DstId(rid=rid, pnc=pid)

    sy.dma_start(T.xs[:], T.x[:]).then_inc(S.ldx, 16)
    act.dma_start(T.ws[:], T.w[:]).then_inc(S.ldw, 16)
    v.memset(T.on1[:], 1.0).then_inc(S.cst, 1)
    g.wait_ge(S.cst, 1)
    g.affine_select(T.idn[:], T.on1[:], [[-1, 128]], A.is_equal, 0.0, 0, 1).then_inc(S.idr, 1)
    act.wait_ge(S.ldx, 16)
    act.activation(T.xq[:], T.xs[:], F.Square).then_inc(S.sq, 1)

    pe.wait_ge(S.cst, 1)
    pe.wait_ge(S.ldx, 16)
    pe.matmul(T.pS[:, 0:1], T.xs[:, 0:128], one, True, True).then_inc(S.pe1, 1)
    pe.matmul(T.pS[:, 1:2], T.xs[:, 128:256], one, True, True).then_inc(S.pe1, 1)
    pe.wait_ge(S.sq, 1)
    pe.matmul(T.pS[:, 2:3], T.xq[:, 0:128], one, True, True).then_inc(S.pe1, 1)
    pe.matmul(T.pS[:, 3:4], T.xq[:, 128:256], one, True, True).then_inc(S.pe1, 1)
    pe.wait_ge(S.ldw, 16)
    pe.matmul(T.pS[:, 4:5], T.ws[:], one, True, True).then_inc(S.pe1, 1)
    pe.matmul(T.pA0[:, 0:128], T.ws[:], T.xs[:, 0:128], True, True).then_inc(S.pa0, 1)
    pe.matmul(T.pA1[:, 0:128], T.ws[:], T.xs[:, 128:256], True, True).then_inc(S.pa1, 1)
    v.wait_ge(S.pe1, 5)
    v.tensor_copy(T.ss[:], T.pS[:, 0:NS]).then_inc(S.sc, 1)
    v.wait_ge(S.pa0, 1)
    v.tensor_copy(T.sb[:, 0:128], T.pA0[:, 0:128]).then_inc(S.mc, 1)
    act.wait_ge(S.pa1, 1)
    act.activation(T.sb[:, 128:256], T.pA1[:, 0:128], F.Copy).then_inc(S.mc, 1)

    g.wait_ge(S.sc, 1)
    g.remote_dma_fused([RemoteDMATransfer(dst_ids=[dst(h) for h in holders[kk]], dma_engine_mask=m, remote_sem=S.s1,
                                          srcs=[T.ss[:]], dsts=[T.l1s[slot] for h in holders[kk]], alu_op=0)
                        for kk, m in ((pk, off), (k, onm))], local_sem=S.snt)
    g.wait_ge(S.mc, 2)
    tr = []
    for kk, m in ((pk, off), (k, onm)):
        for i, h in enumerate(holders[kk]):
            q = (2 * P["pidx"][kk[0]] + i) * W
            tr.append(RemoteDMATransfer(dst_ids=[dst(h)], dma_engine_mask=_part(m, i, 2), remote_sem=S.m1,
                                        srcs=[T.sb[:, q:q + W]], dsts=[T.l1[slot]], alu_op=0))
    g.remote_dma_fused(tr, local_sem=S.snt)

    exp = 0
    for b in P["four"][k[0]]:
        for i, h in enumerate(holders[b]):
            far, near = _stat_dests(P, b, i)
            o, m = _masks(topo, h, P["on"][P["peer"][b]][0], P["on"][b][0])
            exp += len(_bits(o)) * far.count(core) + len(_bits(m)) * near.count(core)
    v.wait_ge(S.st, exp)
    v.tensor_tensor(T.t1[:], T.sp[:, 0:2 * NS], T.sp[:, 2 * NS:4 * NS], A.add).then_inc(S.v1, 1)
    v.wait_ge(S.v1, 1)
    v.tensor_tensor(T.t2[:], T.t1[:, 0:NS], T.t1[:, NS:2 * NS], A.add).then_inc(S.v2, 1)
    v.wait_ge(S.v2, 1)
    v.tensor_scalar(T.mu[:], T.t2[:, 0:2], 1.0 / D, None, A.mult).then_inc(S.v3, 1)
    v.tensor_scalar(T.ve[:], T.t2[:, 2:4], 1.0 / D, EPS, A.mult, A.add).then_inc(S.v4, 1)
    v.wait_ge(S.v3, 1)
    v.tensor_tensor(T.m2[:], T.mu[:], T.mu[:], A.mult).then_inc(S.v5, 1)
    v.wait_ge(S.v4, 1)
    v.wait_ge(S.v5, 1)
    v.tensor_tensor(T.va[:], T.ve[:], T.m2[:], A.subtract).then_inc(S.v6, 1)
    act.wait_ge(S.v6, 1)
    act.activation(T.sd[:], T.va[:], F.Sqrt).then_inc(S.sqd, 1)
    v.wait_ge(S.idr, 1)
    v.tensor_scalar(T.dgm[:, 0:128], T.idn[:], T.mu[:, 0:1], None, A.mult).then_inc(S.dm, 1)
    v.tensor_scalar(T.dgm[:, 128:256], T.idn[:], T.mu[:, 1:2], None, A.mult).then_inc(S.dm, 1)
    pe.wait_ge(S.dm, 2)
    pe.matmul(T.pM[:, 0:TK], T.on1[:], T.dgm[:], True, True).then_inc(S.pm, 1)
    v.wait_ge(S.pm, 1)
    v.tensor_scalar(T.pG[:, 0:TK], T.pM[:, 0:TK], T.t2[:, 4:5], None, A.mult).then_inc(S.vg, 1)
    v.wait_ge(S.sqd, 1)
    v.reciprocal(T.rs[:], T.sd[:]).then_inc(S.rsr, 1)
    v.wait_ge(S.rsr, 1)
    v.tensor_scalar(T.dgr[:, 0:128], T.idn[:], T.rs[:, 0:1], None, A.mult).then_inc(S.dr0, 1)
    act.wait_ge(S.rsr, 1)
    act.wait_ge(S.idr, 1)
    act.activation(T.dgr[:, 128:256], T.idn[:], F.Copy, scale=T.rs[:, 1:2]).then_inc(S.dr1, 1)
    pe.wait_ge(S.dr0, 1)
    pe.matmul(T.pB[:, 0:128], T.on1[:], T.dgr[:, 0:128], True, True).then_inc(S.pb, 1)
    pe.wait_ge(S.dr1, 1)
    pe.matmul(T.pB[:, 128:256], T.on1[:], T.dgr[:, 128:256], True, True).then_inc(S.pb, 1)

    v.wait_ge(S.vg, 1)
    first = True
    for kk, sem, su, sy_, q_, sst in ((k, S.m3a, S.ua, S.ya, sy, S.sta), (pk, S.m3b, S.ub, S.yb, act, S.stb)):
        c0 = 2 * P["pidx"][kk[0]] * W
        c1 = c0 + 2 * W
        n = 0
        for h in holders[kk]:
            o, m = _masks(topo, h, P["on"][P["peer"][kk]][0], P["on"][kk][0])
            n += len(_bits(m if kk == k else o))
        v.wait_ge(sem, n)
        v.tensor_tensor(T.u[:, c0:c1], T.acc[:, c0:c1], T.pG[:, c0:c1], A.subtract).then_inc(su, 1)
        v.wait_ge(su, 1)
        if first:
            v.wait_ge(S.pb, 2)
            first = False
        v.tensor_tensor(T.yo[:, c0:c1], T.u[:, c0:c1], T.pB[:, c0:c1], A.mult).then_inc(sy_, 1)
        q_.wait_ge(sy_, 1)
        q_.dma_start(T.y[:, c0:c1], T.yo[:, c0:c1]).then_inc(sst, 16)
    g.wait_ge(S.snt, 2 * (len(_bits(off)) + len(_bits(onm))))
    g.wait_ge(S.sta, 16)
    g.wait_ge(S.stb, 16)


def rank_program(g, core, T, topo):
    P = _plan(T, topo)
    if T.rank_of(core) is not None:
        _rank(g, core, T, topo, P)
    elif core in P["role"]:
        _holder(g, core, T, topo, P)
